import numpy as np
import ml_dtypes


def mxq(x, axis, fmt="e4m3"):
    dtype, down = {"e4m3": (ml_dtypes.float8_e4m3fn, 7), "e5m2": (ml_dtypes.float8_e5m2, 14)}[fmt]
    v = np.moveaxis(np.asarray(x, np.float32).astype(ml_dtypes.bfloat16).astype(np.float64), axis, -1)
    blocks = v.reshape(v.shape[:-1] + (-1, 32))
    amax = np.abs(blocks).max(-1, keepdims=True)
    byte = np.maximum(np.where(amax > 0, np.frexp(amax)[1] - 1 + 127, 0) - down, 1)
    scale = np.exp2(byte - 127.0)
    codes = (blocks / scale).astype(np.float32).astype(dtype).astype(np.float64)
    return np.moveaxis((codes * scale).reshape(v.shape), -1, axis)


WIDE = False


def mx_kscale(k):
    if not WIDE:
        return np.ones(k)
    levels = np.array([10, -10, 5, -5, 0])
    if k % 512:
        return np.exp2(np.random.permutation(np.resize(levels, k // 32))).repeat(32)
    a = np.empty((k // 512, 16))
    for p in range(k // 512):
        a[p, :8] = np.random.permutation(np.resize(levels, 8))
        for g in range(8):
            far = levels[np.abs(levels - a[p, g]) >= 10]
            a[p, g + 8] = far[np.random.randint(len(far))]
    return np.exp2(a.ravel()).repeat(32)


def f64(x):
    return np.asarray(x).astype(np.float64)


def striped(idx):
    return np.tile(np.asarray(idx).reshape(-1, 16).T, (8, 1)).astype(np.uint16)


def unstriped(offs):
    return offs[:16].T.reshape(-1).astype(np.int64)


E2M1 = np.array([0.0, 0.5, 1.0, 1.5, 2.0, 3.0, 4.0, 6.0, -0.0, -0.5, -1.0, -1.5, -2.0, -3.0, -4.0, -6.0])


def pack_weight(w, fmt):
    k, n = w.shape
    w = f64(np.asarray(w, np.float32).astype(ml_dtypes.bfloat16)).reshape(k // 32, 32, n)
    amax = np.abs(w).max(1)
    if fmt == "e4m3":
        byte = np.frexp(amax)[1] - 1 + 127 - 7
    else:
        mant, ex = np.frexp(amax / 6.0)
        byte = np.where(mant > 0.5, ex, ex - 1) + 127
    byte = np.clip(np.where(amax > 0, byte, 1), 1, 254)
    scaled = (w * np.exp2(127.0 - byte)[:, None, :]).reshape(k, n).astype(np.float32)
    by_word = np.ascontiguousarray(scaled.reshape(k // 512, 128, 4, n).transpose(0, 1, 3, 2))
    if fmt == "e4m3":
        words = by_word.astype(ml_dtypes.float8_e4m3fn).view(np.uint8)
    else:
        c = by_word.astype(ml_dtypes.float4_e2m1fn).view(np.uint8) & 0xF
        words = (c[..., 0::2] | (c[..., 1::2] << 4)).reshape(k // 512, 128, 2 * n)
    return np.ascontiguousarray(words), np.ascontiguousarray(byte.astype(np.uint8).reshape(k // 512, 16, n))


def unpack_weight(words, scales, fmt):
    g, _, n = scales.shape
    words = np.ascontiguousarray(words).reshape(g, 128, n, -1)
    if fmt == "e4m3":
        vals = words.view(ml_dtypes.float8_e4m3fn).astype(np.float64)
    else:
        nib = np.empty((g, 128, n, 4), np.uint8)
        nib[..., 0::2] = words & 0xF
        nib[..., 1::2] = words >> 4
        vals = E2M1[nib]
    vals = vals * np.repeat(np.exp2(scales.astype(np.float64) - 127.0), 8, axis=1)[..., None]
    return vals.transpose(0, 1, 3, 2).reshape(g * 512, n)


def sigmoid(v):
    return 1.0 / (1.0 + np.exp(-v))


D, T, U, I, J = 512, 1024, 1024, 256, 512


def setup_inputs():
    n = np.random.standard_normal
    idx3 = np.random.permutation(J)[:J]
    idx = np.random.permutation(T)[:I]
    idx2 = np.random.permutation(U)[:J]
    fd = mx_kscale(D)
    tabbp = pack_weight(n((D, U)) / fd[:, None], "e2m1")
    return {
        "taba": (n((D, T)) * 1 / np.sqrt(D) * fd[:, None]).astype(np.float32),
        "dtab": (n((D, T)) * 1.3 / np.sqrt(D) * fd[:, None]).astype(np.float32),
        "tabb_words": tabbp[0],
        "tabb_scales": tabbp[1],
        "pw": (np.random.uniform(-1.5, 1.5, (1, J))).astype(np.float32),
        "base": (0.3 * n((I, J))).astype(np.float32),
        "offs3": striped(idx3),
        "offs": striped(idx),
        "offs2": striped(idx2),
    }


def reference(taba, dtab, tabb_words, tabb_scales, pw, base, offs3, offs, offs2):
    idx3 = unstriped(offs3)
    idx = unstriped(offs)
    idx2 = unstriped(offs2)
    tabbu = unpack_weight(tabb_words, tabb_scales, "e2m1")
    tabaidxq = mxq(f64(taba)[:, idx], 0, "e4m3")
    tabbidx2g = tabbu[:, idx2]
    s = tabaidxq.T @ tabbidx2g
    dtabidxq = mxq(f64(dtab)[:, idx], 0, "e4m3")
    ts = dtabidxq.T @ tabbidx2g
    g1 = sigmoid(s)
    e1 = f64(pw) * s
    s1 = np.zeros((I, J))
    s1[:, idx3] = e1
    xg1 = ts * g1 * (1.0 - g1)
    xe1 = ts * f64(pw)
    xs1 = np.zeros((I, J))
    xs1[:, idx3] = xe1
    xds = xg1[:, idx3] * f64(pw) + (xs1 * g1 + xg1 * s1) * (1.0 - g1) + xg1 * (-1.0) * s1 * g1
    y = xds + f64(base)
    return y

@@ -1,0 +1,211 @@
+from contextlib import ExitStack
+
+import concourse.mybir as mybir
+from concourse.masks import make_identity
+
+D, T, U, I, J = 512, 1024, 1024, 256, 512
+FLOPS = 2 * 2 * D * I * J
+
+F32 = mybir.dt.float32
+BF16 = mybir.dt.bfloat16
+I32 = mybir.dt.int32
+U32 = mybir.dt.uint32
+U16 = mybir.dt.uint16
+U8 = mybir.dt.uint8
+FP8X4 = mybir.dt.float8_e4m3fn_x4
+FP4X4 = mybir.dt.float4_e2m1fn_x4
+ACT = mybir.ActivationFunctionType
+ALU = mybir.AluOpType
+
+P = 128
+PACK = 4
+TILES = I // P
+BLOCKS = J // P
+HALF = J // 2
+SCATTER_WINDOW = 704
+
+
+def tile_attend_hvpairlink_kernel(tc, taba, dtab, tabb_words, tabb_scales, pw, base, offs3, offs, offs2, out):
+    nc = tc.nc
+    with ExitStack() as ctx:
+        keep = ctx.enter_context(tc.tile_pool(name="keep", bufs=1))
+        scores = ctx.enter_context(tc.psum_pool(name="scores", bufs=4))
+        turns = ctx.enter_context(tc.psum_pool(name="turns", bufs=4))
+
+        def sb(name, shape, dtype, tag=None):
+            return keep.tile(shape, dtype, name=name, tag=tag or name, align_bytes=64)
+
+        taba_planes = taba.rearrange("(p t) c -> p t c", t=PACK)
+        dtab_planes = dtab.rearrange("(p t) c -> p t c", t=PACK)
+
+        list3 = sb("list3", [P, J // 16], U16)
+        list1 = sb("list1", [P, I // 16], U16)
+        list2 = sb("list2", [P, J // 16], U16)
+        b_words = sb("b_words", [P, U], U16)
+        b_scales = sb("b_scales", [P, U], U8)
+        a01 = sb("a01", [P, 2, T], F32)
+        a2 = sb("a2", [P, T], F32)
+        a3 = sb("a3", [P, T], F32)
+        d_raw = [sb("d_raw%d" % u, [P, 2, T], F32) for u in range(2)]
+        pw_cols = sb("pw_cols", [P, BLOCKS], F32)
+        base_sb = [sb("base%d" % m, [P, J], F32) for m in range(TILES)]
+
+        nc.sync.dma_start(list2[:], offs2)
+        nc.sync.dma_start(b_words[:].bitcast(I32), tabb_words[0].bitcast(I32))
+        for q in range(4):
+            rows = tabb_scales[0, 4 * q : 4 * q + 4, :].bitcast(I32)
+            nc.scalar.dma_start(b_scales[32 * q : 32 * q + 32, :].bitcast(I32), rows.unsqueeze(0).broadcast_to([8, 4, U // 4]))
+        nc.sync.dma_start(list1[:], offs)
+        nc.sync.dma_start(a01[:], taba_planes[:, 0:2, :])
+        nc.sync.dma_start(a2[:], taba_planes[:, 2, :])
+        nc.sync.dma_start(a3[:], taba_planes[:, 3, :])
+        nc.sync.dma_start(pw_cols[:], pw.rearrange("o (n b) -> n (o b)", b=BLOCKS))
+        nc.sync.dma_start(list3[:], offs3)
+        for u in range(2):
+            nc.sync.dma_start(d_raw[u][:], dtab_planes[:, 2 * u : 2 * u + 2, :])
+        for m in range(TILES):
+            nc.sync.dma_start(base_sb[m][:], base[m * P : (m + 1) * P, :])
+
+        ident = sb("ident", [P, P], F32)
+        make_identity(nc, ident[:])
+        warm = sb("warm", [P, 1], F32)
+        nc.scalar.activation(warm[:], ident[:, 0:1], ACT.Tanh)
+
+        pw_bank = turns.tile([P, BLOCKS, P], F32, name="pw_bank", tag="turn")
+        for b in range(BLOCKS):
+            nc.tensor.transpose(pw_bank[:, b, :], pw_cols[:, b : b + 1].to_broadcast([P, P]), ident[:])
+        pw_row = sb("pw_row", [P, J], F32)
+        nc.scalar.copy(pw_row[:].rearrange("p (n b) -> p n b", b=BLOCKS), pw_bank[:].rearrange("p b n -> p n b"))
+
+        bg_words = sb("bg_words", [P, J], U16)
+        bg_scales = sb("bg_scales", [P, J], U8)
+        nc.vector.tensor_copy(bg_words[:], b_words[:].indirect(list2[:]))
+        nc.vector.tensor_copy(bg_scales[:], b_scales[:].indirect(list2[:]))
+
+        def quantise_and_score(name, grouped):
+            banks = []
+            codes = sb(name + "_codes", [P, I], U32)
+            planes = sb(name + "_scales", [P, I], U8)
+            for m in range(TILES):
+                cols = slice(m * P, (m + 1) * P)
+                nc.vector.quantize_mx(
+                    out=codes[:, cols].bitcast(FP8X4), scales=planes[:, cols], in_=grouped[:, m * P * PACK : (m + 1) * P * PACK]
+                )
+            for m in range(TILES):
+                cols = slice(m * P, (m + 1) * P)
+                bank = scores.tile([P, J], F32, name="%s_bank%d" % (name, m), tag="score")
+                nc.tensor.matmul_mx(
+                    out=bank[:],
+                    lhsT=codes[:, cols].bitcast(FP8X4),
+                    lhsT_scale=planes[:, cols],
+                    rhs=bg_words[:].bitcast(FP4X4),
+                    rhs_scale=bg_scales[:],
+                    start=True,
+                    stop=True,
+                )
+                banks.append(bank)
+            return banks
+
+        ag = sb("ag", [P, PACK, I], F32)
+        for t, window in enumerate((a01[:, 0, :], a01[:, 1, :], a2[:], a3[:])):
+            nc.vector.tensor_copy(ag[:, t, :], window.indirect(list1[:]))
+        a_grouped = sb("a_grouped", [P, I * PACK], BF16)
+        for m in range(TILES):
+            nc.vector.tensor_copy(
+                a_grouped[:, m * P * PACK : (m + 1) * P * PACK].rearrange("p (c i t) -> p c t i", i=4, t=PACK),
+                ag[:, :, m * P : (m + 1) * P].rearrange("p t (c i) -> p c t i", i=4),
+            )
+        s_bank = quantise_and_score("a", a_grouped)
+
+        s_sb = [sb("s_sb%d" % m, [P, J], F32) for m in range(TILES)]
+        s1 = [sb("s1_%d" % m, [P, SCATTER_WINDOW], F32) for m in range(TILES)]
+        for m in range(TILES):
+            nc.scalar.copy(s_sb[m][:], s_bank[m][:])
+            nc.vector.tensor_tensor(s1[m][:].indirect(list3[:]), s_sb[m][:], pw_row[:], ALU.mult)
+
+        d_grouped = sb("d_grouped", [P, I * PACK], BF16)
+        dg = sb("dg", [P, 2, I], U32)
+        for u in range(2):
+            pairs = sb("d_pairs%d" % u, [P, 2 * T], BF16)
+            nc.scalar.activation(pairs[:].rearrange("p (c e) -> p c e", e=2), d_raw[u][:].rearrange("p e c -> p c e"), ACT.Copy)
+            nc.vector.tensor_copy(dg[:, u, :], pairs[:].bitcast(U32).indirect(list1[:]))
+        nc.vector.tensor_copy(
+            d_grouped[:].bitcast(I32).rearrange("p (c u) -> p c u", u=2), dg[:].bitcast(I32).rearrange("p u c -> p c u")
+        )
+        ts_bank = quantise_and_score("d", d_grouped)
+
+        h = [sb("h%d" % m, [P, J], F32) for m in range(TILES)]
+        slope = [sb("slope%d" % m, [P, J], F32) for m in range(TILES)]
+        hs1_both = sb("hs1", [P, TILES, J], F32, "d_grouped")
+        hs1 = [hs1_both[:, m, :] for m in range(TILES)]
+        for m in range(TILES):
+            nc.scalar.activation(h[m][:], s_bank[m][:], ACT.Tanh, scale=0.5)
+            nc.vector.tensor_tensor(hs1[m], h[m][:], s1[m][:, 0:J], ALU.mult)
+        for m in range(TILES):
+            quarter_sq = sb("quarter_sq%d" % m, [P, J], F32)
+            nc.scalar.activation(quarter_sq[:], h[m][:], ACT.Square, scale=0.5)
+            nc.scalar.activation(slope[m][:], quarter_sq[:], ACT.Copy, scale=-1.0, bias=0.25)
+
+        ts_sb = [sb("ts_sb%d" % m, [P, J], F32) for m in range(TILES)]
+        xs1 = {}
+        for m in range(TILES):
+            nc.scalar.copy(ts_sb[m][:], ts_bank[m][:])
+
+        def scatter_xe1(m, tag):
+            xs1[m] = sb("xs1_%d" % m, [P, SCATTER_WINDOW], F32, tag)
+            nc.vector.tensor_tensor(xs1[m][:].indirect(list3[:]), ts_sb[m][:], pw_row[:], ALU.mult)
+
+        def linked_terms(m):
+            xg1 = sb("xg1_%d" % m, [P, J], F32)
+            nc.vector.tensor_tensor(xg1[:], ts_bank[m][:], slope[m][:], ALU.mult)
+            return xg1
+
+        def curvature_terms(m, xg1):
+            bend = sb("bend%d" % m, [P, J], F32)
+            nc.vector.scalar_tensor_tensor(bend[:], hs1[m], -1.0, xg1[:], ALU.mult, ALU.mult)
+            linked = sb("linked%d" % m, [P, J], F32)
+            for e in range(2):
+                cols = slice(e * HALF, (e + 1) * HALF)
+                nc.vector.tensor_tensor(
+                    linked[:, cols], xg1[:].indirect(list3[:, e * HALF // 16 : (e + 1) * HALF // 16]), pw_row[:, cols], ALU.mult
+                )
+            return [bend, linked]
+
+        def add_on_tensor(m, terms):
+            turned = turns.tile([P, J], F32, name="turned%d" % m, tag="turn")
+            for b in range(BLOCKS):
+                cols = slice(b * P, (b + 1) * P)
+                for n, term in enumerate(terms):
+                    nc.tensor.matmul(
+                        turned[:, cols], term[:, cols], ident[:], start=(n == 0), stop=(n == len(terms) - 1), is_transpose=True
+                    )
+            turned_sb = sb("turned_sb%d" % m, [P, J], F32)
+            nc.scalar.copy(turned_sb[:], turned[:])
+            back = turns.tile([P, J], F32, name="back%d" % m, tag="turn")
+            for b in range(BLOCKS):
+                cols = slice(b * P, (b + 1) * P)
+                nc.tensor.transpose(back[:, cols], turned_sb[:, cols], ident[:])
+            return back
+
+        xg1 = [linked_terms(m) for m in range(TILES)]
+        scatter_xe1(0, None)
+        first = curvature_terms(0, xg1[0])
+        direct0 = sb("direct0", [P, J], F32)
+        nc.vector.tensor_tensor(direct0[:], xs1[0][:, 0:J], slope[0][:], ALU.mult)
+        total = add_on_tensor(0, [base_sb[0], direct0] + first)
+        last = curvature_terms(1, xg1[1])
+        rest = add_on_tensor(1, [base_sb[1]] + last)
+        result0 = sb("result0", [P, J], F32)
+        nc.scalar.copy(result0[:], total[:])
+        nc.sync.dma_start(out[0:P, :], result0[:])
+
+        scatter_xe1(1, "xg1_1")
+        direct1 = sb("direct1", [P, J], F32)
+        result1 = sb("result1", [P, J], F32)
+        for e in range(2):
+            cols = slice(e * HALF, (e + 1) * HALF)
+            nc.vector.tensor_tensor(direct1[:, cols], xs1[1][:, cols], slope[1][:, cols], ALU.mult)
+        for e in range(2):
+            cols = slice(e * HALF, (e + 1) * HALF)
+            nc.vector.tensor_tensor(result1[:, cols], rest[:, cols], direct1[:, cols], ALU.add)
+            nc.sync.dma_start(out[P : 2 * P, cols], result1[:, cols])

@@ -29,8 +29,7 @@ def tile_attend_hvpairlink_kernel(tc, taba, dtab, tabb_words, tabb_scales, pw, b
     nc = tc.nc
     with ExitStack() as ctx:
         keep = ctx.enter_context(tc.tile_pool(name="keep", bufs=1))
-        scores = ctx.enter_context(tc.psum_pool(name="scores", bufs=4))
-        turns = ctx.enter_context(tc.psum_pool(name="turns", bufs=4))
+        psum = ctx.enter_context(tc.psum_pool(name="psum", bufs=8))
 
         def sb(name, shape, dtype, tag=None):
             return keep.tile(shape, dtype, name=name, tag=tag or name, align_bytes=64)
@@ -57,9 +56,9 @@ def tile_attend_hvpairlink_kernel(tc, taba, dtab, tabb_words, tabb_scales, pw, b
             nc.scalar.dma_start(b_scales[32 * q : 32 * q + 32, :].bitcast(I32), rows.unsqueeze(0).broadcast_to([8, 4, U // 4]))
         nc.sync.dma_start(list1[:], offs)
         nc.sync.dma_start(a01[:], taba_planes[:, 0:2, :])
+        nc.sync.dma_start(pw_cols[:], pw.rearrange("o (n b) -> n (o b)", b=BLOCKS))
         nc.sync.dma_start(a2[:], taba_planes[:, 2, :])
         nc.sync.dma_start(a3[:], taba_planes[:, 3, :])
-        nc.sync.dma_start(pw_cols[:], pw.rearrange("o (n b) -> n (o b)", b=BLOCKS))
         nc.sync.dma_start(list3[:], offs3)
         for u in range(2):
             nc.sync.dma_start(d_raw[u][:], dtab_planes[:, 2 * u : 2 * u + 2, :])
@@ -71,80 +70,96 @@ def tile_attend_hvpairlink_kernel(tc, taba, dtab, tabb_words, tabb_scales, pw, b
         warm = sb("warm", [P, 1], F32)
         nc.scalar.activation(warm[:], ident[:, 0:1], ACT.Tanh)
 
-        pw_bank = turns.tile([P, BLOCKS, P], F32, name="pw_bank", tag="turn")
+        pw_bank = psum.tile([P, BLOCKS, P], F32, name="pw_bank", tag="bank")
         for b in range(BLOCKS):
             nc.tensor.transpose(pw_bank[:, b, :], pw_cols[:, b : b + 1].to_broadcast([P, P]), ident[:])
         pw_row = sb("pw_row", [P, J], F32)
         nc.scalar.copy(pw_row[:].rearrange("p (n b) -> p n b", b=BLOCKS), pw_bank[:].rearrange("p b n -> p n b"))
 
-        bg_words = sb("bg_words", [P, J], U16)
-        bg_scales = sb("bg_scales", [P, J], U8)
-        nc.vector.tensor_copy(bg_words[:], b_words[:].indirect(list2[:]))
-        nc.vector.tensor_copy(bg_scales[:], b_scales[:].indirect(list2[:]))
+        def half_of(lst, e):
+            width = lst.shape[1] // 2
+            return lst[:, e * width : (e + 1) * width]
 
-        def quantise_and_score(name, grouped):
-            banks = []
+        bg_words = sb("bg_words", [P, J], U16)
+        nc.vector.tensor_copy(bg_words[:], b_words[:].indirect(list2[:]))
+        bg_scales = [sb("bg_scales0", [P, HALF], U8)]
+        nc.vector.tensor_copy(bg_scales[0][:], b_scales[:].indirect(half_of(list2, 0)))
+
+        def quantise(name, grouped, width):
             codes = sb(name + "_codes", [P, I], U32)
             planes = sb(name + "_scales", [P, I], U8)
-            for m in range(TILES):
-                cols = slice(m * P, (m + 1) * P)
+            for c0 in range(0, I, width):
+                cols = slice(c0, c0 + width)
                 nc.vector.quantize_mx(
-                    out=codes[:, cols].bitcast(FP8X4), scales=planes[:, cols], in_=grouped[:, m * P * PACK : (m + 1) * P * PACK]
+                    out=codes[:, cols].bitcast(FP8X4), scales=planes[:, cols], in_=grouped[:, c0 * PACK : (c0 + width) * PACK]
                 )
-            for m in range(TILES):
-                cols = slice(m * P, (m + 1) * P)
-                bank = scores.tile([P, J], F32, name="%s_bank%d" % (name, m), tag="score")
-                nc.tensor.matmul_mx(
-                    out=bank[:],
-                    lhsT=codes[:, cols].bitcast(FP8X4),
-                    lhsT_scale=planes[:, cols],
-                    rhs=bg_words[:].bitcast(FP4X4),
-                    rhs_scale=bg_scales[:],
-                    start=True,
-                    stop=True,
-                )
-                banks.append(bank)
-            return banks
+            return codes, planes
 
-        ag = sb("ag", [P, PACK, I], F32)
-        for t, window in enumerate((a01[:, 0, :], a01[:, 1, :], a2[:], a3[:])):
+        def score(dst, quantised, m, e):
+            codes, planes = quantised
+            cols = slice(m * P, (m + 1) * P)
+            nc.tensor.matmul_mx(
+                out=dst,
+                lhsT=codes[:, cols].bitcast(FP8X4),
+                lhsT_scale=planes[:, cols],
+                rhs=bg_words[:, e * HALF : (e + 1) * HALF].bitcast(FP4X4),
+                rhs_scale=bg_scales[e][:],
+                start=True,
+                stop=True,
+            )
+
+        ag = sb("ag", [P, PACK - 1, I], F32)
+        for t, window in enumerate((a01[:, 0, :], a01[:, 1, :], a2[:])):
             nc.vector.tensor_copy(ag[:, t, :], window.indirect(list1[:]))
         a_grouped = sb("a_grouped", [P, I * PACK], BF16)
+        nc.vector.tensor_copy(
+            a_grouped[:].rearrange("p (c i t) -> p c t i", i=4, t=PACK)[:, :, 0 : PACK - 1, :],
+            ag[:].rearrange("p t (c i) -> p c t i", i=4),
+        )
+        last_place = a_grouped[:].rearrange("p (c t) -> p c t", t=PACK)[:, :, PACK - 1]
         for m in range(TILES):
-            nc.vector.tensor_copy(
-                a_grouped[:, m * P * PACK : (m + 1) * P * PACK].rearrange("p (c i t) -> p c t i", i=4, t=PACK),
-                ag[:, :, m * P : (m + 1) * P].rearrange("p t (c i) -> p c t i", i=4),
-            )
-        s_bank = quantise_and_score("a", a_grouped)
+            nc.vector.tensor_copy(last_place[:, m * P : (m + 1) * P], a3[:].indirect(half_of(list1, m)))
+        a_quantised = quantise("a", a_grouped, P)
+        bg_scales.append(sb("bg_scales1", [P, HALF], U8, "a_grouped"))
+        nc.vector.tensor_copy(bg_scales[1][:], b_scales[:].indirect(half_of(list2, 1)))
 
         s_sb = [sb("s_sb%d" % m, [P, J], F32) for m in range(TILES)]
-        s1 = [sb("s1_%d" % m, [P, SCATTER_WINDOW], F32) for m in range(TILES)]
-        for m in range(TILES):
-            nc.scalar.copy(s_sb[m][:], s_bank[m][:])
-            nc.vector.tensor_tensor(s1[m][:].indirect(list3[:]), s_sb[m][:], pw_row[:], ALU.mult)
+        s1 = [sb("s1_%d" % m, [P, J], F32) for m in range(TILES)]
+        for e in range(2):
+            cols = slice(e * HALF, (e + 1) * HALF)
+            for m in range(TILES):
+                bank = psum.tile([P, HALF], F32, name="s_bank%d%d" % (m, e), tag="bank")
+                score(bank[:], a_quantised, m, e)
+                nc.scalar.copy(s_sb[m][:, cols], bank[:])
+                nc.vector.tensor_tensor(s1[m][:].indirect(half_of(list3, e)), s_sb[m][:, cols], pw_row[:, cols], ALU.mult)
 
         d_grouped = sb("d_grouped", [P, I * PACK], BF16)
         dg = sb("dg", [P, 2, I], U32)
-        for u in range(2):
-            pairs = sb("d_pairs%d" % u, [P, 2 * T], BF16)
+        for u, tag in enumerate(("a_codes", None)):
+            pairs = sb("d_pairs%d" % u, [P, 2 * T], BF16, tag)
             nc.scalar.activation(pairs[:].rearrange("p (c e) -> p c e", e=2), d_raw[u][:].rearrange("p e c -> p c e"), ACT.Copy)
             nc.vector.tensor_copy(dg[:, u, :], pairs[:].bitcast(U32).indirect(list1[:]))
         nc.vector.tensor_copy(
             d_grouped[:].bitcast(I32).rearrange("p (c u) -> p c u", u=2), dg[:].bitcast(I32).rearrange("p u c -> p c u")
         )
-        ts_bank = quantise_and_score("d", d_grouped)
+        d_quantised = quantise("d", d_grouped, I)
+        ts_bank = []
+        for m in range(TILES):
+            bank = psum.tile([P, J], F32, name="ts_bank%d" % m, tag="bank")
+            for e in range(2):
+                score(bank[:, e * HALF : (e + 1) * HALF], d_quantised, m, e)
+            ts_bank.append(bank)
 
         h = [sb("h%d" % m, [P, J], F32) for m in range(TILES)]
         slope = [sb("slope%d" % m, [P, J], F32) for m in range(TILES)]
         hs1_both = sb("hs1", [P, TILES, J], F32, "d_grouped")
         hs1 = [hs1_both[:, m, :] for m in range(TILES)]
         for m in range(TILES):
-            nc.scalar.activation(h[m][:], s_bank[m][:], ACT.Tanh, scale=0.5)
-            nc.vector.tensor_tensor(hs1[m], h[m][:], s1[m][:, 0:J], ALU.mult)
-        for m in range(TILES):
+            nc.scalar.activation(h[m][:], s_sb[m][:], ACT.Tanh, scale=0.5)
             quarter_sq = sb("quarter_sq%d" % m, [P, J], F32)
             nc.scalar.activation(quarter_sq[:], h[m][:], ACT.Square, scale=0.5)
             nc.scalar.activation(slope[m][:], quarter_sq[:], ACT.Copy, scale=-1.0, bias=0.25)
+            nc.vector.tensor_tensor(hs1[m], h[m][:], s1[m][:], ALU.mult)
 
         ts_sb = [sb("ts_sb%d" % m, [P, J], F32) for m in range(TILES)]
         xs1 = {}
@@ -160,8 +175,8 @@ def tile_attend_hvpairlink_kernel(tc, taba, dtab, tabb_words, tabb_scales, pw, b
             nc.vector.tensor_tensor(xg1[:], ts_bank[m][:], slope[m][:], ALU.mult)
             return xg1
 
-        def curvature_terms(m, xg1):
-            bend = sb("bend%d" % m, [P, J], F32)
+        def curvature_terms(m, xg1, tag):
+            bend = sb("bend%d" % m, [P, J], F32, tag)
             nc.vector.scalar_tensor_tensor(bend[:], hs1[m], -1.0, xg1[:], ALU.mult, ALU.mult)
             linked = sb("linked%d" % m, [P, J], F32)
             for e in range(2):
@@ -171,35 +186,39 @@ def tile_attend_hvpairlink_kernel(tc, taba, dtab, tabb_words, tabb_scales, pw, b
                 )
             return [bend, linked]
 
-        def add_on_tensor(m, terms):
-            turned = turns.tile([P, J], F32, name="turned%d" % m, tag="turn")
-            for b in range(BLOCKS):
+        def turn_and_add(name, terms):
+            bank = psum.tile([P, HALF], F32, name=name, tag="bank")
+            for b in range(BLOCKS // 2):
                 cols = slice(b * P, (b + 1) * P)
                 for n, term in enumerate(terms):
                     nc.tensor.matmul(
-                        turned[:, cols], term[:, cols], ident[:], start=(n == 0), stop=(n == len(terms) - 1), is_transpose=True
+                        bank[:, cols], term[:, cols], ident[:], start=(n == 0), stop=(n == len(terms) - 1), is_transpose=True
                     )
-            turned_sb = sb("turned_sb%d" % m, [P, J], F32)
-            nc.scalar.copy(turned_sb[:], turned[:])
-            back = turns.tile([P, J], F32, name="back%d" % m, tag="turn")
-            for b in range(BLOCKS):
-                cols = slice(b * P, (b + 1) * P)
-                nc.tensor.transpose(back[:, cols], turned_sb[:, cols], ident[:])
-            return back
+            return bank
+
+        def turned_sum(name, e, terms):
+            bank = turn_and_add(name, [term[:, e * HALF : (e + 1) * HALF] for term in terms])
+            turned = sb(name + "_sb", [P, HALF], F32)
+            nc.scalar.copy(turned[:], bank[:])
+            return turned[:]
 
         xg1 = [linked_terms(m) for m in range(TILES)]
-        scatter_xe1(0, None)
-        first = curvature_terms(0, xg1[0])
+        last = curvature_terms(1, xg1[1], None)
+        rest = [turn_and_add("rest%d" % e, [turned_sum("early1%d" % e, e, [base_sb[1]] + last)]) for e in range(2)]
+        scatter_xe1(0, "xg1_1")
+        first = curvature_terms(0, xg1[0], None)
+        early = [turned_sum("early0%d" % e, e, [base_sb[0]] + first) for e in range(2)]
         direct0 = sb("direct0", [P, J], F32)
         nc.vector.tensor_tensor(direct0[:], xs1[0][:, 0:J], slope[0][:], ALU.mult)
-        total = add_on_tensor(0, [base_sb[0], direct0] + first)
-        last = curvature_terms(1, xg1[1])
-        rest = add_on_tensor(1, [base_sb[1]] + last)
+        late = [turned_sum("late0%d" % e, e, [direct0]) for e in range(2)]
         result0 = sb("result0", [P, J], F32)
-        nc.scalar.copy(result0[:], total[:])
-        nc.sync.dma_start(out[0:P, :], result0[:])
+        for e in range(2):
+            cols = slice(e * HALF, (e + 1) * HALF)
+            total = turn_and_add("total%d" % e, [early[e], late[e]])
+            nc.scalar.copy(result0[:, cols], total[:])
+            nc.scalar.dma_start(out[0:P, cols], result0[:, cols])
 
-        scatter_xe1(1, "xg1_1")
+        scatter_xe1(1, "xg1_0")
         direct1 = sb("direct1", [P, J], F32)
         result1 = sb("result1", [P, J], F32)
         for e in range(2):
@@ -207,5 +226,5 @@ def tile_attend_hvpairlink_kernel(tc, taba, dtab, tabb_words, tabb_scales, pw, b
             nc.vector.tensor_tensor(direct1[:, cols], xs1[1][:, cols], slope[1][:, cols], ALU.mult)
         for e in range(2):
             cols = slice(e * HALF, (e + 1) * HALF)
-            nc.vector.tensor_tensor(result1[:, cols], rest[:, cols], direct1[:, cols], ALU.add)
+            nc.vector.tensor_tensor(result1[:, cols], rest[e][:], direct1[:, cols], ALU.add)
             nc.sync.dma_start(out[P : 2 * P, cols], result1[:, cols])

@@ -19,49 +19,62 @@ ALU = mybir.AluOpType
 
 P = 128
 PACK = 4
+GROUP = 16
+QUADRANT = 32
+SCALE_ROWS = 4
+LINE = 4
+PSUM_BANKS = 8
 TILES = I // P
 BLOCKS = J // P
 HALF = J // 2
-SCATTER_WINDOW = 704
+WIDE = 704
 
 
 def tile_attend_hvpairlink_kernel(tc, taba, dtab, tabb_words, tabb_scales, pw, base, offs3, offs, offs2, out):
     nc = tc.nc
     with ExitStack() as ctx:
         keep = ctx.enter_context(tc.tile_pool(name="keep", bufs=1))
-        psum = ctx.enter_context(tc.psum_pool(name="psum", bufs=8))
+        psum = ctx.enter_context(tc.psum_pool(name="psum", bufs=PSUM_BANKS))
 
-        def sb(name, shape, dtype, tag=None):
-            return keep.tile(shape, dtype, name=name, tag=tag or name, align_bytes=64)
+        def sb(name, shape, dtype, after=None):
+            return keep.tile(shape, dtype, name=name, tag=after or name, align_bytes=64)
+
+        def half_cols(e):
+            return slice(e * HALF, (e + 1) * HALF)
+
+        def half_list(listed, e):
+            width = listed.shape[1] // 2
+            return listed[:, e * width : (e + 1) * width]
 
         taba_planes = taba.rearrange("(p t) c -> p t c", t=PACK)
         dtab_planes = dtab.rearrange("(p t) c -> p t c", t=PACK)
-
-        list3 = sb("list3", [P, J // 16], U16)
-        list1 = sb("list1", [P, I // 16], U16)
-        list2 = sb("list2", [P, J // 16], U16)
+        idx3 = sb("idx3", [P, J // GROUP], U16)
+        idx = sb("idx", [P, I // GROUP], U16)
+        idx2 = sb("idx2", [P, J // GROUP], U16)
         b_words = sb("b_words", [P, U], U16)
         b_scales = sb("b_scales", [P, U], U8)
-        a01 = sb("a01", [P, 2, T], F32)
-        a2 = sb("a2", [P, T], F32)
-        a3 = sb("a3", [P, T], F32)
-        d_raw = [sb("d_raw%d" % u, [P, 2, T], F32) for u in range(2)]
+        a_plane = [sb("a_plane%d" % t, [P, T], F32) for t in range(PACK)]
+        d_planes = [sb("d_planes%d" % u, [P, 2, T], F32) for u in range(2)]
         pw_cols = sb("pw_cols", [P, BLOCKS], F32)
         base_sb = [sb("base%d" % m, [P, J], F32) for m in range(TILES)]
 
-        nc.sync.dma_start(list2[:], offs2)
+        nc.sync.dma_start(idx2[:], offs2)
         nc.sync.dma_start(b_words[:].bitcast(I32), tabb_words[0].bitcast(I32))
-        for q in range(4):
-            rows = tabb_scales[0, 4 * q : 4 * q + 4, :].bitcast(I32)
-            nc.scalar.dma_start(b_scales[32 * q : 32 * q + 32, :].bitcast(I32), rows.unsqueeze(0).broadcast_to([8, 4, U // 4]))
-        nc.sync.dma_start(list1[:], offs)
-        nc.sync.dma_start(a01[:], taba_planes[:, 0:2, :])
+        for q in range(P // QUADRANT):
+            rows = tabb_scales[0, SCALE_ROWS * q : SCALE_ROWS * (q + 1), :].bitcast(I32)
+            nc.scalar.dma_start(
+                b_scales[QUADRANT * q : QUADRANT * (q + 1), :].bitcast(I32),
+                rows.unsqueeze(0).broadcast_to([QUADRANT // SCALE_ROWS, SCALE_ROWS, rows.shape[1]]),
+            )
+        nc.sync.dma_start(idx[:], offs)
+        for t in range(2):
+            nc.sync.dma_start(a_plane[t][:], taba_planes[:, t, :])
         nc.sync.dma_start(pw_cols[:], pw.rearrange("o (n b) -> n (o b)", b=BLOCKS))
-        nc.sync.dma_start(a2[:], taba_planes[:, 2, :])
-        nc.sync.dma_start(a3[:], taba_planes[:, 3, :])
-        nc.sync.dma_start(list3[:], offs3)
+        for t in range(2, PACK):
+            nc.sync.dma_start(a_plane[t][:], taba_planes[:, t, :])
+        nc.sync.dma_start(idx3[:], offs3)
         for u in range(2):
-            nc.sync.dma_start(d_raw[u][:], dtab_planes[:, 2 * u : 2 * u + 2, :])
+            nc.sync.dma_start(d_planes[u][:], dtab_planes[:, 2 * u : 2 * u + 2, :])
         for m in range(TILES):
             nc.sync.dma_start(base_sb[m][:], base[m * P : (m + 1) * P, :])
 
@@ -76,69 +89,66 @@ def tile_attend_hvpairlink_kernel(tc, taba, dtab, tabb_words, tabb_scales, pw, b
         pw_row = sb("pw_row", [P, J], F32)
         nc.scalar.copy(pw_row[:].rearrange("p (n b) -> p n b", b=BLOCKS), pw_bank[:].rearrange("p b n -> p n b"))
 
-        def half_of(lst, e):
-            width = lst.shape[1] // 2
-            return lst[:, e * width : (e + 1) * width]
-
         bg_words = sb("bg_words", [P, J], U16)
-        nc.vector.tensor_copy(bg_words[:], b_words[:].indirect(list2[:]))
+        nc.vector.tensor_copy(bg_words[:], b_words[:].indirect(idx2[:]))
         bg_scales = [sb("bg_scales0", [P, HALF], U8)]
-        nc.vector.tensor_copy(bg_scales[0][:], b_scales[:].indirect(half_of(list2, 0)))
+        nc.vector.tensor_copy(bg_scales[0][:], b_scales[:].indirect(half_list(idx2, 0)))
 
         def quantise(name, grouped, width):
             codes = sb(name + "_codes", [P, I], U32)
-            planes = sb(name + "_scales", [P, I], U8)
+            scales = sb(name + "_scales", [P, I], U8)
             for c0 in range(0, I, width):
                 cols = slice(c0, c0 + width)
                 nc.vector.quantize_mx(
-                    out=codes[:, cols].bitcast(FP8X4), scales=planes[:, cols], in_=grouped[:, c0 * PACK : (c0 + width) * PACK]
+                    out=codes[:, cols].bitcast(FP8X4), scales=scales[:, cols], in_=grouped[:, c0 * PACK : (c0 + width) * PACK]
                 )
-            return codes, planes
+            return codes, scales
 
         def score(dst, quantised, m, e):
-            codes, planes = quantised
+            codes, scales = quantised
             cols = slice(m * P, (m + 1) * P)
             nc.tensor.matmul_mx(
                 out=dst,
                 lhsT=codes[:, cols].bitcast(FP8X4),
-                lhsT_scale=planes[:, cols],
-                rhs=bg_words[:, e * HALF : (e + 1) * HALF].bitcast(FP4X4),
+                lhsT_scale=scales[:, cols],
+                rhs=bg_words[:, half_cols(e)].bitcast(FP4X4),
                 rhs_scale=bg_scales[e][:],
                 start=True,
                 stop=True,
             )
 
-        ag = sb("ag", [P, PACK - 1, I], F32)
-        for t, window in enumerate((a01[:, 0, :], a01[:, 1, :], a2[:])):
-            nc.vector.tensor_copy(ag[:, t, :], window.indirect(list1[:]))
+        ag = sb("ag", [P, 2, I], F32)
+        for t in range(2):
+            nc.vector.tensor_copy(ag[:, t, :], a_plane[t][:].indirect(idx[:]))
         a_grouped = sb("a_grouped", [P, I * PACK], BF16)
         nc.vector.tensor_copy(
-            a_grouped[:].rearrange("p (c i t) -> p c t i", i=4, t=PACK)[:, :, 0 : PACK - 1, :],
-            ag[:].rearrange("p t (c i) -> p c t i", i=4),
+            a_grouped[:].rearrange("p (c n t) -> p c t n", n=LINE, t=PACK)[:, :, 0:2, :],
+            ag[:].rearrange("p t (c n) -> p c t n", n=LINE),
         )
-        last_place = a_grouped[:].rearrange("p (c t) -> p c t", t=PACK)[:, :, PACK - 1]
+        a_places = a_grouped[:].rearrange("p (c t) -> p c t", t=PACK)
+        nc.vector.tensor_copy(a_places[:, :, 2], a_plane[2][:].indirect(idx[:]))
         for m in range(TILES):
-            nc.vector.tensor_copy(last_place[:, m * P : (m + 1) * P], a3[:].indirect(half_of(list1, m)))
+            nc.vector.tensor_copy(a_places[:, m * P : (m + 1) * P, 3], a_plane[3][:].indirect(half_list(idx, m)))
         a_quantised = quantise("a", a_grouped, P)
-        bg_scales.append(sb("bg_scales1", [P, HALF], U8, "a_grouped"))
-        nc.vector.tensor_copy(bg_scales[1][:], b_scales[:].indirect(half_of(list2, 1)))
+        bg_scales.append(sb("bg_scales1", [P, HALF], U8, after="a_grouped"))
+        nc.vector.tensor_copy(bg_scales[1][:], b_scales[:].indirect(half_list(idx2, 1)))
 
         s_sb = [sb("s_sb%d" % m, [P, J], F32) for m in range(TILES)]
         s1 = [sb("s1_%d" % m, [P, J], F32) for m in range(TILES)]
         for e in range(2):
-            cols = slice(e * HALF, (e + 1) * HALF)
+            cols = half_cols(e)
             for m in range(TILES):
                 bank = psum.tile([P, HALF], F32, name="s_bank%d%d" % (m, e), tag="bank")
                 score(bank[:], a_quantised, m, e)
                 nc.scalar.copy(s_sb[m][:, cols], bank[:])
-                nc.vector.tensor_tensor(s1[m][:].indirect(half_of(list3, e)), s_sb[m][:, cols], pw_row[:, cols], ALU.mult)
+                nc.vector.tensor_tensor(s1[m][:].indirect(half_list(idx3, e)), s_sb[m][:, cols], pw_row[:, cols], ALU.mult)
 
         d_grouped = sb("d_grouped", [P, I * PACK], BF16)
         dg = sb("dg", [P, 2, I], U32)
-        for u, tag in enumerate(("a_codes", None)):
-            pairs = sb("d_pairs%d" % u, [P, 2 * T], BF16, tag)
-            nc.scalar.activation(pairs[:].rearrange("p (c e) -> p c e", e=2), d_raw[u][:].rearrange("p e c -> p c e"), ACT.Copy)
-            nc.vector.tensor_copy(dg[:, u, :], pairs[:].bitcast(U32).indirect(list1[:]))
+        for u, after in enumerate(("a_codes", None)):
+            pairs = sb("d_pairs%d" % u, [P, 2 * T], BF16, after)
+            nc.scalar.activation(pairs[:].rearrange("p (c t) -> p c t", t=2), d_planes[u][:].rearrange("p t c -> p c t"), ACT.Copy)
+            nc.vector.tensor_copy(dg[:, u, :], pairs[:].bitcast(U32).indirect(idx[:]))
         nc.vector.tensor_copy(
             d_grouped[:].bitcast(I32).rearrange("p (c u) -> p c u", u=2), dg[:].bitcast(I32).rearrange("p u c -> p c u")
         )
@@ -147,48 +157,40 @@ def tile_attend_hvpairlink_kernel(tc, taba, dtab, tabb_words, tabb_scales, pw, b
         for m in range(TILES):
             bank = psum.tile([P, J], F32, name="ts_bank%d" % m, tag="bank")
             for e in range(2):
-                score(bank[:, e * HALF : (e + 1) * HALF], d_quantised, m, e)
+                score(bank[:, half_cols(e)], d_quantised, m, e)
             ts_bank.append(bank)
 
         h = [sb("h%d" % m, [P, J], F32) for m in range(TILES)]
         slope = [sb("slope%d" % m, [P, J], F32) for m in range(TILES)]
-        hs1_both = sb("hs1", [P, TILES, J], F32, "d_grouped")
-        hs1 = [hs1_both[:, m, :] for m in range(TILES)]
+        hs1 = sb("hs1", [P, TILES, J], F32, after="d_grouped")
         for m in range(TILES):
             nc.scalar.activation(h[m][:], s_sb[m][:], ACT.Tanh, scale=0.5)
-            quarter_sq = sb("quarter_sq%d" % m, [P, J], F32)
-            nc.scalar.activation(quarter_sq[:], h[m][:], ACT.Square, scale=0.5)
-            nc.scalar.activation(slope[m][:], quarter_sq[:], ACT.Copy, scale=-1.0, bias=0.25)
-            nc.vector.tensor_tensor(hs1[m], h[m][:], s1[m][:], ALU.mult)
+            half_h_sq = sb("half_h_sq%d" % m, [P, J], F32)
+            nc.scalar.activation(half_h_sq[:], h[m][:], ACT.Square, scale=0.5)
+            nc.scalar.activation(slope[m][:], half_h_sq[:], ACT.Copy, scale=-1.0, bias=0.25)
+            nc.vector.tensor_tensor(hs1[:, m, :], h[m][:], s1[m][:], ALU.mult)
 
         ts_sb = [sb("ts_sb%d" % m, [P, J], F32) for m in range(TILES)]
-        xs1 = {}
         for m in range(TILES):
             nc.scalar.copy(ts_sb[m][:], ts_bank[m][:])
 
-        def scatter_xe1(m, tag):
-            xs1[m] = sb("xs1_%d" % m, [P, SCATTER_WINDOW], F32, tag)
-            nc.vector.tensor_tensor(xs1[m][:].indirect(list3[:]), ts_sb[m][:], pw_row[:], ALU.mult)
+        def scatter_xe1(m, after):
+            xs1 = sb("xs1_%d" % m, [P, WIDE], F32, after)
+            nc.vector.tensor_tensor(xs1[:].indirect(idx3[:]), ts_sb[m][:], pw_row[:], ALU.mult)
+            return xs1
 
-        def linked_terms(m):
-            xg1 = sb("xg1_%d" % m, [P, J], F32)
-            nc.vector.tensor_tensor(xg1[:], ts_bank[m][:], slope[m][:], ALU.mult)
-            return xg1
-
-        def curvature_terms(m, xg1, tag):
-            bend = sb("bend%d" % m, [P, J], F32, tag)
-            nc.vector.scalar_tensor_tensor(bend[:], hs1[m], -1.0, xg1[:], ALU.mult, ALU.mult)
+        def bend_and_linked(m):
+            bend = sb("bend%d" % m, [P, J], F32)
+            nc.vector.scalar_tensor_tensor(bend[:], hs1[:, m, :], -1.0, xg1[m][:], ALU.mult, ALU.mult)
             linked = sb("linked%d" % m, [P, J], F32)
             for e in range(2):
-                cols = slice(e * HALF, (e + 1) * HALF)
-                nc.vector.tensor_tensor(
-                    linked[:, cols], xg1[:].indirect(list3[:, e * HALF // 16 : (e + 1) * HALF // 16]), pw_row[:, cols], ALU.mult
-                )
+                cols = half_cols(e)
+                nc.vector.tensor_tensor(linked[:, cols], xg1[m][:].indirect(half_list(idx3, e)), pw_row[:, cols], ALU.mult)
             return [bend, linked]
 
         def turn_and_add(name, terms):
             bank = psum.tile([P, HALF], F32, name=name, tag="bank")
-            for b in range(BLOCKS // 2):
+            for b in range(HALF // P):
                 cols = slice(b * P, (b + 1) * P)
                 for n, term in enumerate(terms):
                     nc.tensor.matmul(
@@ -197,34 +199,39 @@ def tile_attend_hvpairlink_kernel(tc, taba, dtab, tabb_words, tabb_scales, pw, b
             return bank
 
         def turned_sum(name, e, terms):
-            bank = turn_and_add(name, [term[:, e * HALF : (e + 1) * HALF] for term in terms])
+            bank = turn_and_add(name, [term[:, half_cols(e)] for term in terms])
             turned = sb(name + "_sb", [P, HALF], F32)
             nc.scalar.copy(turned[:], bank[:])
             return turned[:]
 
-        xg1 = [linked_terms(m) for m in range(TILES)]
-        last = curvature_terms(1, xg1[1], None)
-        rest = [turn_and_add("rest%d" % e, [turned_sum("early1%d" % e, e, [base_sb[1]] + last)]) for e in range(2)]
-        scatter_xe1(0, "xg1_1")
-        first = curvature_terms(0, xg1[0], None)
-        early = [turned_sum("early0%d" % e, e, [base_sb[0]] + first) for e in range(2)]
+        xg1 = []
+        for m in range(TILES):
+            xg1.append(sb("xg1_%d" % m, [P, J], F32))
+            nc.vector.tensor_tensor(xg1[m][:], ts_bank[m][:], slope[m][:], ALU.mult)
+
+        terms1 = [base_sb[1]] + bend_and_linked(1)
+        rest1 = [turn_and_add("rest1%d" % e, [turned_sum("early1%d" % e, e, terms1)]) for e in range(2)]
+
+        xs1_0 = scatter_xe1(0, after="xg1_1")
+        terms0 = [base_sb[0]] + bend_and_linked(0)
+        early0 = [turned_sum("early0%d" % e, e, terms0) for e in range(2)]
         direct0 = sb("direct0", [P, J], F32)
-        nc.vector.tensor_tensor(direct0[:], xs1[0][:, 0:J], slope[0][:], ALU.mult)
-        late = [turned_sum("late0%d" % e, e, [direct0]) for e in range(2)]
+        nc.vector.tensor_tensor(direct0[:], xs1_0[:, 0:J], slope[0][:], ALU.mult)
+        late0 = [turned_sum("late0%d" % e, e, [direct0]) for e in range(2)]
         result0 = sb("result0", [P, J], F32)
         for e in range(2):
-            cols = slice(e * HALF, (e + 1) * HALF)
-            total = turn_and_add("total%d" % e, [early[e], late[e]])
+            cols = half_cols(e)
+            total = turn_and_add("total0%d" % e, [early0[e], late0[e]])
             nc.scalar.copy(result0[:, cols], total[:])
             nc.scalar.dma_start(out[0:P, cols], result0[:, cols])
 
-        scatter_xe1(1, "xg1_0")
+        xs1_1 = scatter_xe1(1, after="xg1_0")
         direct1 = sb("direct1", [P, J], F32)
         result1 = sb("result1", [P, J], F32)
         for e in range(2):
-            cols = slice(e * HALF, (e + 1) * HALF)
-            nc.vector.tensor_tensor(direct1[:, cols], xs1[1][:, cols], slope[1][:, cols], ALU.mult)
+            cols = half_cols(e)
+            nc.vector.tensor_tensor(direct1[:, cols], xs1_1[:, cols], slope[1][:, cols], ALU.mult)
         for e in range(2):
-            cols = slice(e * HALF, (e + 1) * HALF)
-            nc.vector.tensor_tensor(result1[:, cols], rest[e][:], direct1[:, cols], ALU.add)
+            cols = half_cols(e)
+            nc.vector.tensor_tensor(result1[:, cols], rest1[e][:], direct1[:, cols], ALU.add)
             nc.sync.dma_start(out[P : 2 * P, cols], result1[:, cols])

from contextlib import ExitStack

import concourse.mybir as mybir
from concourse.masks import make_identity

D, T, U, I, J = 512, 1024, 1024, 256, 512
FLOPS = 2 * 2 * D * I * J

F32 = mybir.dt.float32
BF16 = mybir.dt.bfloat16
I32 = mybir.dt.int32
U32 = mybir.dt.uint32
U16 = mybir.dt.uint16
U8 = mybir.dt.uint8
FP8X4 = mybir.dt.float8_e4m3fn_x4
FP4X4 = mybir.dt.float4_e2m1fn_x4
ACT = mybir.ActivationFunctionType
ALU = mybir.AluOpType

P = 128
PACK = 4
GROUP = 16
QUADRANT = 32
SCALE_ROWS = 4
LINE = 4
PSUM_BANKS = 8
TILES = I // P
BLOCKS = J // P
HALF = J // 2
WIDE = 704


def tile_attend_hvpairlink_kernel(tc, taba, dtab, tabb_words, tabb_scales, pw, base, offs3, offs, offs2, out):
    nc = tc.nc
    with ExitStack() as ctx:
        keep = ctx.enter_context(tc.tile_pool(name="keep", bufs=1))
        psum = ctx.enter_context(tc.psum_pool(name="psum", bufs=PSUM_BANKS))

        def sb(name, shape, dtype, after=None):
            return keep.tile(shape, dtype, name=name, tag=after or name, align_bytes=64)

        def half_cols(e):
            return slice(e * HALF, (e + 1) * HALF)

        def half_list(listed, e):
            width = listed.shape[1] // 2
            return listed[:, e * width : (e + 1) * width]

        taba_planes = taba.rearrange("(p t) c -> p t c", t=PACK)
        dtab_planes = dtab.rearrange("(p t) c -> p t c", t=PACK)
        idx3 = sb("idx3", [P, J // GROUP], U16)
        idx = sb("idx", [P, I // GROUP], U16)
        idx2 = sb("idx2", [P, J // GROUP], U16)
        b_words = sb("b_words", [P, U], U16)
        b_scales = sb("b_scales", [P, U], U8)
        a_plane = [sb("a_plane%d" % t, [P, T], F32) for t in range(PACK)]
        d_planes = [sb("d_planes%d" % u, [P, 2, T], F32) for u in range(2)]
        pw_cols = sb("pw_cols", [P, BLOCKS], F32)
        base_sb = [sb("base%d" % m, [P, J], F32) for m in range(TILES)]

        nc.sync.dma_start(idx2[:], offs2)
        nc.sync.dma_start(b_words[:].bitcast(I32), tabb_words[0].bitcast(I32))
        for q in range(P // QUADRANT):
            rows = tabb_scales[0, SCALE_ROWS * q : SCALE_ROWS * (q + 1), :].bitcast(I32)
            nc.scalar.dma_start(
                b_scales[QUADRANT * q : QUADRANT * (q + 1), :].bitcast(I32),
                rows.unsqueeze(0).broadcast_to([QUADRANT // SCALE_ROWS, SCALE_ROWS, rows.shape[1]]),
            )
        nc.sync.dma_start(idx[:], offs)
        for t in range(2):
            nc.sync.dma_start(a_plane[t][:], taba_planes[:, t, :])
        nc.sync.dma_start(pw_cols[:], pw.rearrange("o (n b) -> n (o b)", b=BLOCKS))
        for t in range(2, PACK):
            nc.sync.dma_start(a_plane[t][:], taba_planes[:, t, :])
        nc.sync.dma_start(idx3[:], offs3)
        for u in range(2):
            nc.sync.dma_start(d_planes[u][:], dtab_planes[:, 2 * u : 2 * u + 2, :])
        for m in range(TILES):
            nc.sync.dma_start(base_sb[m][:], base[m * P : (m + 1) * P, :])

        ident = sb("ident", [P, P], F32)
        make_identity(nc, ident[:])
        warm = sb("warm", [P, 1], F32)
        nc.scalar.activation(warm[:], ident[:, 0:1], ACT.Tanh)

        pw_bank = psum.tile([P, BLOCKS, P], F32, name="pw_bank", tag="bank")
        for b in range(BLOCKS):
            nc.tensor.transpose(pw_bank[:, b, :], pw_cols[:, b : b + 1].to_broadcast([P, P]), ident[:])
        pw_row = sb("pw_row", [P, J], F32)
        nc.scalar.copy(pw_row[:].rearrange("p (n b) -> p n b", b=BLOCKS), pw_bank[:].rearrange("p b n -> p n b"))

        bg_words = sb("bg_words", [P, J], U16)
        nc.vector.tensor_copy(bg_words[:], b_words[:].indirect(idx2[:]))
        bg_scales = [sb("bg_scales0", [P, HALF], U8)]
        nc.vector.tensor_copy(bg_scales[0][:], b_scales[:].indirect(half_list(idx2, 0)))

        def quantise(name, grouped, width):
            codes = sb(name + "_codes", [P, I], U32)
            scales = sb(name + "_scales", [P, I], U8)
            for c0 in range(0, I, width):
                cols = slice(c0, c0 + width)
                nc.vector.quantize_mx(
                    out=codes[:, cols].bitcast(FP8X4), scales=scales[:, cols], in_=grouped[:, c0 * PACK : (c0 + width) * PACK]
                )
            return codes, scales

        def score(dst, quantised, m, e):
            codes, scales = quantised
            cols = slice(m * P, (m + 1) * P)
            nc.tensor.matmul_mx(
                out=dst,
                lhsT=codes[:, cols].bitcast(FP8X4),
                lhsT_scale=scales[:, cols],
                rhs=bg_words[:, half_cols(e)].bitcast(FP4X4),
                rhs_scale=bg_scales[e][:],
                start=True,
                stop=True,
            )

        ag = sb("ag", [P, 2, I], F32)
        for t in range(2):
            nc.vector.tensor_copy(ag[:, t, :], a_plane[t][:].indirect(idx[:]))
        a_grouped = sb("a_grouped", [P, I * PACK], BF16)
        nc.vector.tensor_copy(
            a_grouped[:].rearrange("p (c n t) -> p c t n", n=LINE, t=PACK)[:, :, 0:2, :],
            ag[:].rearrange("p t (c n) -> p c t n", n=LINE),
        )
        a_places = a_grouped[:].rearrange("p (c t) -> p c t", t=PACK)
        nc.vector.tensor_copy(a_places[:, :, 2], a_plane[2][:].indirect(idx[:]))
        for m in range(TILES):
            nc.vector.tensor_copy(a_places[:, m * P : (m + 1) * P, 3], a_plane[3][:].indirect(half_list(idx, m)))
        a_quantised = quantise("a", a_grouped, P)
        bg_scales.append(sb("bg_scales1", [P, HALF], U8, after="a_grouped"))
        nc.vector.tensor_copy(bg_scales[1][:], b_scales[:].indirect(half_list(idx2, 1)))

        s_sb = [sb("s_sb%d" % m, [P, J], F32) for m in range(TILES)]
        s1 = [sb("s1_%d" % m, [P, J], F32) for m in range(TILES)]
        for e in range(2):
            cols = half_cols(e)
            for m in range(TILES):
                bank = psum.tile([P, HALF], F32, name="s_bank%d%d" % (m, e), tag="bank")
                score(bank[:], a_quantised, m, e)
                nc.scalar.copy(s_sb[m][:, cols], bank[:])
                nc.vector.tensor_tensor(s1[m][:].indirect(half_list(idx3, e)), s_sb[m][:, cols], pw_row[:, cols], ALU.mult)

        d_grouped = sb("d_grouped", [P, I * PACK], BF16)
        dg = sb("dg", [P, 2, I], U32)
        for u, after in enumerate(("a_codes", None)):
            pairs = sb("d_pairs%d" % u, [P, 2 * T], BF16, after)
            nc.scalar.activation(pairs[:].rearrange("p (c t) -> p c t", t=2), d_planes[u][:].rearrange("p t c -> p c t"), ACT.Copy)
            nc.vector.tensor_copy(dg[:, u, :], pairs[:].bitcast(U32).indirect(idx[:]))
        nc.vector.tensor_copy(
            d_grouped[:].bitcast(I32).rearrange("p (c u) -> p c u", u=2), dg[:].bitcast(I32).rearrange("p u c -> p c u")
        )
        d_quantised = quantise("d", d_grouped, I)
        ts_bank = []
        for m in range(TILES):
            bank = psum.tile([P, J], F32, name="ts_bank%d" % m, tag="bank")
            for e in range(2):
                score(bank[:, half_cols(e)], d_quantised, m, e)
            ts_bank.append(bank)

        h = [sb("h%d" % m, [P, J], F32) for m in range(TILES)]
        slope = [sb("slope%d" % m, [P, J], F32) for m in range(TILES)]
        hs1 = sb("hs1", [P, TILES, J], F32, after="d_grouped")
        for m in range(TILES):
            nc.scalar.activation(h[m][:], s_sb[m][:], ACT.Tanh, scale=0.5)
            half_h_sq = sb("half_h_sq%d" % m, [P, J], F32)
            nc.scalar.activation(half_h_sq[:], h[m][:], ACT.Square, scale=0.5)
            nc.scalar.activation(slope[m][:], half_h_sq[:], ACT.Copy, scale=-1.0, bias=0.25)
            nc.vector.tensor_tensor(hs1[:, m, :], h[m][:], s1[m][:], ALU.mult)

        ts_sb = [sb("ts_sb%d" % m, [P, J], F32) for m in range(TILES)]
        for m in range(TILES):
            nc.scalar.copy(ts_sb[m][:], ts_bank[m][:])

        def scatter_xe1(m, after):
            xs1 = sb("xs1_%d" % m, [P, WIDE], F32, after)
            nc.vector.tensor_tensor(xs1[:].indirect(idx3[:]), ts_sb[m][:], pw_row[:], ALU.mult)
            return xs1

        def bend_and_linked(m):
            bend = sb("bend%d" % m, [P, J], F32)
            nc.vector.scalar_tensor_tensor(bend[:], hs1[:, m, :], -1.0, xg1[m][:], ALU.mult, ALU.mult)
            linked = sb("linked%d" % m, [P, J], F32)
            for e in range(2):
                cols = half_cols(e)
                nc.vector.tensor_tensor(linked[:, cols], xg1[m][:].indirect(half_list(idx3, e)), pw_row[:, cols], ALU.mult)
            return [bend, linked]

        def turn_and_add(name, terms):
            bank = psum.tile([P, HALF], F32, name=name, tag="bank")
            for b in range(HALF // P):
                cols = slice(b * P, (b + 1) * P)
                for n, term in enumerate(terms):
                    nc.tensor.matmul(
                        bank[:, cols], term[:, cols], ident[:], start=(n == 0), stop=(n == len(terms) - 1), is_transpose=True
                    )
            return bank

        def turned_sum(name, e, terms):
            bank = turn_and_add(name, [term[:, half_cols(e)] for term in terms])
            turned = sb(name + "_sb", [P, HALF], F32)
            nc.scalar.copy(turned[:], bank[:])
            return turned[:]

        xg1 = []
        for m in range(TILES):
            xg1.append(sb("xg1_%d" % m, [P, J], F32))
            nc.vector.tensor_tensor(xg1[m][:], ts_bank[m][:], slope[m][:], ALU.mult)

        terms1 = [base_sb[1]] + bend_and_linked(1)
        rest1 = [turn_and_add("rest1%d" % e, [turned_sum("early1%d" % e, e, terms1)]) for e in range(2)]

        xs1_0 = scatter_xe1(0, after="xg1_1")
        terms0 = [base_sb[0]] + bend_and_linked(0)
        early0 = [turned_sum("early0%d" % e, e, terms0) for e in range(2)]
        direct0 = sb("direct0", [P, J], F32)
        nc.vector.tensor_tensor(direct0[:], xs1_0[:, 0:J], slope[0][:], ALU.mult)
        late0 = [turned_sum("late0%d" % e, e, [direct0]) for e in range(2)]
        result0 = sb("result0", [P, J], F32)
        for e in range(2):
            cols = half_cols(e)
            total = turn_and_add("total0%d" % e, [early0[e], late0[e]])
            nc.scalar.copy(result0[:, cols], total[:])
            nc.scalar.dma_start(out[0:P, cols], result0[:, cols])

        xs1_1 = scatter_xe1(1, after="xg1_0")
        direct1 = sb("direct1", [P, J], F32)
        result1 = sb("result1", [P, J], F32)
        for e in range(2):
            cols = half_cols(e)
            nc.vector.tensor_tensor(direct1[:, cols], xs1_1[:, cols], slope[1][:, cols], ALU.mult)
        for e in range(2):
            cols = half_cols(e)
            nc.vector.tensor_tensor(result1[:, cols], rest1[e][:], direct1[:, cols], ALU.add)
            nc.sync.dma_start(out[P : 2 * P, cols], result1[:, cols])
